import numpy as np, ml_dtypes
CORES = [35,38,43,46]
N = 4
import mx_ref
BF = ml_dtypes.bfloat16
def cols(t, e):
    v = np.concatenate([t.reshape(128, -1, 4), np.zeros((128, 1, 4), BF)], axis=1)
    return np.ascontiguousarray(v[:, e]).reshape(128, -1)
def cut(t, i, w=512):
    return t[:, w * i:w * i + w]
def f(rng, *shape):
    return mx_ref.flush((rng.standard_normal(shape, dtype=np.float32) * np.exp2(rng.integers(-2, 3, shape[:-1] + (1,)))).astype(BF))
def wide(rng, *shape, cols=0):
    v = rng.standard_normal(shape, dtype=np.float32) * np.exp2(rng.integers(-12, 13, shape)).astype(np.float32)
    if cols: v *= np.repeat(np.exp2(rng.integers(-cols, cols + 1, shape[:-2] + (1, shape[-1] // 4))) * (rng.random(shape[:-2] + (1, shape[-1] // 4)) > 0.0625), 4, axis=-1).astype(np.float32)
    return mx_ref.flush(v.astype(BF))
T, CAPP = 512, 48
def normal(rng, *shape):
    return mx_ref.flush(rng.standard_normal(shape, dtype=np.float32).astype(BF))
def once(rng, case):
    g = wide if case == "spread" else normal
    c = g(rng, N, 128, 4 * T).transpose(1, 0, 2).reshape(128, N * T, 4)
    v = (wide if case == "spread" else f)(rng, N, 128, 4 * T)
    if case in ("near", "ties"):
        e = np.stack([q * T + rng.permutation(T) for q in range(N)])
        m = T // 16; s = int(rng.integers(1, N))
        sets = [(e[:, :2 * m], np.roll(e[:, 2 * m:4 * m], -s, axis=0)),
                (e[:, 4 * m:7 * m], e[:, 7 * m:10 * m]),
                (e[:, 10 * m:11 * m], e[:, 11 * m:12 * m], e[:, 12 * m:13 * m]),
                (e[:, 13 * m:14 * m], e[:, 14 * m:15 * m], np.roll(e[:, 15 * m:], -s, axis=0))]
        first, at, place = np.zeros(N * T, int), np.zeros(N * T, int), rng.integers(0, 512, N * T)
        for l in sets:
            l = np.sort(np.stack(l), axis=0)
            for i in range(len(l)):
                first[l[i]] = l[0]; at[l[i]] = i; place[l[i]] = place[l[0]]
        c = c[:, first]
        if case == "near": c[place // 4, np.arange(N * T), place % 4] = (1 + 0.25 * at).astype(BF)
    if case == "negative":
        z = normal(rng, 128, 1, 4).astype(np.float32) * np.float32(2.0 ** 20)
        c = mx_ref.flush((c.astype(np.float32) * np.float32(2.0 ** 20) + z).astype(BF))
    an, fb = [], []
    for r in range(N):
        if case == "ties":
            n = rng.permutation([CAPP, CAPP, 128 - 2 * CAPP, 0]); to = []
            for q in range(N):
                w = rng.choice(q * T + np.flatnonzero(at[q * T:q * T + T] < 2), n[q])
                w[:12] = w[:1]; to += list(w)
            to = np.array(to)
        else:
            n = 24 + rng.multinomial(32, np.full(N, np.divide(1, N)))
            while n.max() > 40: n = 24 + rng.multinomial(32, np.full(N, np.divide(1, N)))
            to = np.repeat(np.arange(N) * T, n) + rng.integers(0, T, 128)
        to = rng.permutation(to)
        other = (to + rng.integers(1, N * T, 128)) % (N * T)
        away = (to + rng.integers(1, N * T, 128)) % (N * T)
        h = rng.permutation(128) < (128 if case == "forbid" else 64 if case in ("plain", "spread") else 0)
        best, second = np.where(h, other, to), np.where(h, to, other)
        ban = np.where(h, other, away)
        if case == "ties": ban = np.where(at[to] > 0, first[to], away)
        t = c[:, best].astype(np.float32) + np.float32(0.5) * c[:, second].astype(np.float32)
        if case == "negative": t = t - np.float32(4.5) * z
        if case == "near":
            t[place[to] // 4, np.arange(128), place[to] % 4] = np.where(at[to] > 0, 1, -1) * np.exp2(-rng.integers(1, 6, 128))
        an.append(mx_ref.flush(t.astype(BF)).reshape(128, 512)); fb.append(ban.astype(np.int32).reshape(128, 1))
    k = np.ascontiguousarray(c.reshape(128, N, 4 * T).transpose(1, 0, 2))
    return {"an": np.stack(an), "k": k, "v": v, "u": f(rng, N, 128, 512), "fb": np.stack(fb)}
def planted(d, case):
    if case not in ("near", "negative", "ties"): return True
    s = scores(d["an"], d["k"])
    if case == "negative": return bool((s < 0).all())
    s = allowed(s, d["fb"])
    if case == "near":
        top = np.partition(s, N * T - 2, axis=1)[:, -2:]
        gap = top[:, 1] - top[:, 0]
        return bool(((gap > 0) & (gap < 2.0 ** -9 * np.abs(top[:, 1]))).sum(axis=1).min() >= 20)
    w = np.argmax(s, axis=1)
    per = (s == s.max(axis=1, keepdims=True)).reshape(N, N, T, 128).sum(axis=2)
    within = np.take_along_axis(per, (w // T)[:, None], axis=1)[:, 0] > 1
    across = (per > 0).sum(axis=1) > 1
    return bool(within.sum(axis=1).min() >= 10 and across.sum() >= 20)
def draw(rng, case):
    for _ in range(50):
        d = once(rng, case)
        if not check_inputs(d) and planted(d, case): return d
    raise RuntimeError("no draw in 50 tries: " + case)
def setup_inputs(rng):
    return draw(rng, "plain")
def setup_inputs_forbid(rng):
    return draw(rng, "forbid")
def setup_inputs_near(rng):
    return draw(rng, "near")
def setup_inputs_negative(rng):
    return draw(rng, "negative")
def setup_inputs_spread(rng):
    return draw(rng, "spread")
def setup_inputs_ties(rng):
    return draw(rng, "ties")
def scores(an, k):
    kq = [mx_ref.quantize(cut(k[q], j)) for q in range(N) for j in range(T // 128)]
    out = []
    for r in range(N):
        a = mx_ref.quantize(an[r])
        out.append(np.concatenate([mx_ref.matmul(b, a) for b in kq]))
    return np.stack(out)
def allowed(s, fb):
    for r in range(N): s[r][fb[r][:, 0], np.arange(128)] = -np.inf
    return s
def winners(an, k, fb):
    return np.argmax(allowed(scores(an, k), fb), axis=1)
def check_inputs(d):
    if d["fb"].min() < 0 or d["fb"].max() >= N * T: return ["fb"]
    b = []; w = winners(d["an"], d["k"], d["fb"])
    for r in range(N):
        if np.bincount(w[r] // T, minlength=N).max() > CAPP: b.append("winners")
    return b
def reference(an, k, v, u, fb):
    w = winners(an, k, fb)
    allv = np.concatenate([v[q] for q in range(N)], axis=1)
    y = np.zeros((N, 128, 128), np.float32)
    for r in range(N):
        y[r] = mx_ref.matmul(mx_ref.quantize(u[r]), mx_ref.quantize(cols(allv, w[r])))
    return {"y": y, "win": w.astype(np.float32).reshape(N, 128, 1)}

from concourse.bass import DstId, RemoteDMATransfer
from concourse.mybir import dt, AluOpType, ActivationFunctionType, AxisListType

N, T_K = 4, 512
BIG = 2.0 ** 96
FAR = 4096.0
F8 = "float8_e4m3fn_x4"
W_Y = T_K + 3 * 128

SCRATCH = {
    "an_sb": ("sbuf", [128, 512], "bfloat16"),
    "k_sb": ("sbuf", [128, 2048], "bfloat16"),
    "v_sb": ("sbuf", [128, 2048], "bfloat16"),
    "u_sb": ("sbuf", [128, 512], "bfloat16"),
    "aq": ("sbuf", [128, 512], F8), "asc": ("sbuf", [128, 512], "uint8"),
    "kq": ("sbuf", [128, 512], F8), "ksc": ("sbuf", [128, 512], "uint8"),
    "vq": ("sbuf", [128, 512], F8), "vsc": ("sbuf", [128, 512], "uint8"),
    "uq": ("sbuf", [128, 128], F8), "usc": ("sbuf", [128, 128], "uint8"),
    "hq": ("sbuf", [128, 384], F8), "hsc": ("sbuf", [128, 384], "uint8"),
    "zq": ("sbuf", [128, 512], F8), "zsc": ("sbuf", [128, 512], "uint8"),
    "h_off": ("sbuf", [128, 1024], "bfloat16"),
    "h_on": ("sbuf", [128, 512], "bfloat16"),
    "fbl": ("sbuf", [128, 4], "int32"),
    "fbo": ("sbuf", [128, 4], "float32"),
    "fbf": ("sbuf", [128, 4], "float32"),
    "ones": ("sbuf", [128, 512], "float32"),
    "num": ("sbuf", [128, 512], "float32"),
    "mtmp": ("sbuf", [128, 512], "float32"),
    "pm": ("sbuf", [128, 8], "float32"), "pa": ("sbuf", [128, 8], "float32"),
    "pb": ("sbuf", [128, 8], "float32"), "hm": ("sbuf", [128, 8], "float32"),
    "xa": ("sbuf", [128, 32], "float32"), "xb": ("sbuf", [128, 32], "float32"),
    "base4": ("sbuf", [128, 4], "float32"), "offs": ("sbuf", [128, 4], "float32"),
    "lmi": ("sbuf", [128, 16], "float32"),
    "wm": ("sbuf", [128, 4], "float32"), "pen": ("sbuf", [128, 4], "float32"),
    "gn": ("sbuf", [128, 4], "float32"), "cand": ("sbuf", [128, 4], "float32"),
    "cano": ("sbuf", [128, 4], "float32"), "winr": ("sbuf", [128, 4], "float32"),
    "osel": ("sbuf", [128, 4], "float32"),
    "yw": ("sbuf", [128, W_Y], "float32"),
    "ysb": ("sbuf", [128, 128], "float32"),
    "ps_v": ("psum", [128, 512], "float32"),
}
for _q in range(N):
    SCRATCH["mask%d" % _q] = ("sbuf", [128, 512], "float32")
    SCRATCH["t%d" % _q] = ("sbuf", [128, 512], "float32")
    SCRATCH["cm%d" % _q] = ("sbuf", [128, 516], "float32")
    SCRATCH["junk%d" % _q] = ("sbuf", [128, 512], "bfloat16")
    SCRATCH["ps_s%d" % _q] = ("psum", [128, 512], "float32")
for _q in range(N - 1):
    SCRATCH["ps_y%d" % _q] = ("psum", [128, 512], "float32")
for _s in ("a", "b"):
    for _n in ("r", "d", "e", "f", "g"):
        SCRATCH["c%s_%s" % (_n, _s)] = ("sbuf", [128, 32], "float32")
    SCRATCH["off_%s" % _s] = ("sbuf", [128, 32], "uint16")

N_LOCAL = 110
SEMAPHORES = (["l%d" % _i for _i in range(N_LOCAL)] + ["fb_in", "mi_in", "sent"]
              + ["an_in%d" % _q for _q in range(N)] + ["z_in%d" % _q for _q in range(N)])


def rank_program(g, core, T, topo):
    me = T.rank_of(core)
    if me is None:
        return
    V, S, P, Y = g.vector, g.scalar, g.tensor, g.sync
    A, F = AluOpType, ActivationFunctionType
    u8 = dt.uint8

    used = [0]

    def tok():
        s = T.sem["l%d" % used[0]]
        used[0] += 1
        return {"sem": s, "n": 0, "seen": []}

    def far(sem, n):
        return {"sem": sem, "n": n, "seen": []}

    def inc(call, t, n=1):
        call.then_inc(t["sem"], n)
        t["n"] += n

    def wait(e, name, *ts):
        for t in ts:
            if (name, t["n"]) not in t["seen"]:
                t["seen"].append((name, t["n"]))
                e.wait_ge(t["sem"], t["n"])

    def one(call, n=1):
        t = tok()
        inc(call, t, n)
        return t

    others = [q for q in range(N) if q != me]
    on = [q for q in others if topo.chip(T.cores[q]) == topo.chip(core)]
    off = [q for q in others if q not in on]
    eng_off = topo.engines(core, T.cores[off[0]])
    eng_on = [e for e in topo.engines(core, T.cores[on[0]]) if e not in eng_off]

    def bits(es):
        return sum(1 << e for e in es)

    def did(q):
        a = topo.addr(T.cores[q])
        return DstId(rid=a[0], pnc=a[1])

    sent = [0]

    def send(parts):
        tr = []
        for dst, es, src, lands, sem in parts:
            tr.append(RemoteDMATransfer(dst_ids=[did(q) for q in dst], dma_engine_mask=bits(es), remote_sem=sem,
                                        srcs=[src], dsts=lands))
            sent[0] += len(es)
        g.remote_dma_fused(tr, local_sem=T.sem.sent)

    half = len(eng_off) // 2
    eh = [eng_off[:half], eng_off[half:]]
    W = [128 * q for q in range(N)]
    base_w = [128 * q if q <= me else 128 * q + T_K - 128 for q in range(N)]

    l_an = one(Y.dma_start(T.an_sb[:], T.an[:]), 16)
    l_fb = one(S.dma_start(T.fbl[:, me:me + 1], T.fb[:]), 16)
    l_k = one(Y.dma_start(T.k_sb[:], T.k[:]), 16)

    c_pm = one(g.iota(T.pm[:], [[-16, 8]], 0, 1, allow_small_or_imprecise_dtypes=True))
    c_of = tok()
    inc(g.iota(T.base4[:], [[T_K, N]], 0, 0, allow_small_or_imprecise_dtypes=True), c_of)
    if me > 0:
        inc(g.iota(T.offs[:, 0:me], [[128, me]], 0, 1, allow_small_or_imprecise_dtypes=True), c_of)
    if me < N - 1:
        inc(g.iota(T.offs[:, me + 1:N], [[128, N - 1 - me]], base_w[me + 1], 1, allow_small_or_imprecise_dtypes=True), c_of)

    c1 = one(V.memset(T.ones[:], 1.0))
    c_z = tok()
    inc(V.memset(T.xa[:], 0.0), c_z)
    inc(V.memset(T.xb[:], 0.0), c_z)
    wait(V, "V", c1)
    c_num = one(V.tensor_tensor_scan(T.num[:], T.ones[:], T.ones[:], float(T_K * me - 1), A.mult, A.add))

    wait(V, "V", l_an)
    q_an = one(V.quantize_mx(T.aq[:, W[me]:W[me] + 128], T.asc[:, W[me]:W[me] + 128], T.an_sb[:]))

    wait(g, "g", l_fb)
    fcol = T.fbl[:, me:me + 1]
    send([(off, eng_off, fcol, [fcol] * len(off), T.sem.fb_in), (on, eng_on, fcol, [fcol] * len(on), T.sem.fb_in)])
    wait(g, "g", q_an)
    own_c = T.aq[:, W[me]:W[me] + 128].bitcast(u8)
    own_s = T.asc[:, W[me]:W[me] + 128]
    an_sem = T.sem["an_in%d" % me]
    for src in (own_c, own_s):
        send([(off, eng_off, src, [src] * len(off), an_sem), (on, eng_on, src, [src] * len(on), an_sem)])
    issued = tok()
    g.sem_inc(issued["sem"], 1)
    issued["n"] += 1
    wait(Y, "Y", issued)
    l_v = one(Y.dma_start(T.v_sb[:], T.v[:]), 16)
    l_u = one(Y.dma_start(T.u_sb[:], T.u[:]), 16)

    wait(V, "V", c_pm)
    c_pab = tok()
    inc(V.tensor_scalar(T.pa[:], T.pm[:], -0.5, None, A.is_gt), c_pab)
    inc(V.tensor_scalar(T.pb[:], T.pm[:], 15.5, None, A.is_lt), c_pab)
    wait(V, "V", l_fb)
    v_fbo = one(V.tensor_copy(T.fbo[:, me:me + 1], fcol))
    wait(V, "V", c_pab)
    c_hm = one(V.tensor_tensor(T.hm[:], T.pa[:], T.pb[:], A.mult))
    masks = {}
    wait(V, "V", v_fbo, c_num)
    masks[me] = one(V.tensor_scalar(T["mask%d" % me][:], T.num[:], T.fbo[:, me:me + 1], BIG, A.is_equal, A.mult))
    wait(V, "V", l_k)
    q_k = one(V.quantize_mx(T.kq[:], T.ksc[:], T.k_sb[:]))

    order = [me] + on + off
    scored = {}
    wait(P, "P", q_an, q_k)
    for q in order:
        if q != me:
            wait(P, "P", far(T.sem["an_in%d" % q], 2 * (len(eng_on) if q in on else len(eng_off))))
        scored[q] = one(P.matmul_mx(T["ps_s%d" % q][:], T.aq[:, W[q]:W[q] + 128], T.asc[:, W[q]:W[q] + 128],
                                    T.kq[:], T.ksc[:], True, True))

    scanned, number = {}, {}

    def score(q):
        wait(V, "V", masks[q], scored[q])
        tt = T["t%d" % q]
        a = one(V.tensor_tensor(tt[:], T["ps_s%d" % q][:], T["mask%d" % q][:], A.subtract))
        wait(V, "V", a)
        scanned[q] = one(V.tensor_tensor_scan(T["cm%d" % q][:, 0:T_K], tt[:], tt[:], -2.0 * BIG, A.max, A.max))

    def count(q):
        wait(S, "S", scanned[q])
        cm = T["cm%d" % q]
        number[q] = one(S.activation(T["junk%d" % q][:], cm[:, 0:T_K], F.Sign, bias=cm[:, T_K - 1:T_K], scale=-1.0,
                                     accum_out=cm[:, T_K:T_K + 1]))

    score(me)
    wait(V, "V", far(T.sem.fb_in, sum(len(eng_on) if q in on else len(eng_off) for q in others)))
    v_fbf = one(V.tensor_copy(T.fbf[:], T.fbl[:]))
    wait(V, "V", v_fbf)
    for q in on + off[:1]:
        masks[q] = one(V.tensor_scalar(T["mask%d" % q][:], T.num[:], T.fbf[:, q:q + 1], BIG, A.is_equal, A.mult))

    count(me)
    lq = off[-1]
    wait(S, "S", v_fbf, c_num)
    s1 = one(S.activation(T.mtmp[:], T.num[:], F.Abs, bias=T.fbf[:, lq:lq + 1], scale=-1.0))
    wait(S, "S", s1)
    masks[lq] = one(S.activation(T["mask%d" % lq][:], T.mtmp[:], F.Relu, bias=BIG, scale=-BIG))

    for q in on + off:
        score(q)
        count(q)

    wait(g, "g", *[scanned[q] for q in off + on], *[number[q] for q in off + on])
    land = T.lmi[:, 4 * me:4 * me + 2]
    mi = T.sem.mi_in
    send([([q], es, T["cm%d" % q][:, T_K - 1:T_K + 1], [land], mi) for q, es in zip(off + on, eh + [eng_on])])

    lists = off + on
    wait(V, "V", c_hm, c_z)
    xt = tok()

    def spread(i):
        q = lists[i]
        wait(V, "V", number[q])
        inc(V.tensor_scalar(T.xa[:, 8 * i:8 * i + 8], T.hm[:], T["cm%d" % q][:, T_K:T_K + 1], 4.0, A.mult, A.mult), xt)

    for i in sorted(range(len(lists)), key=lambda i: lists[i] == lq):
        if lists[i] == lq:
            wait(V, "V", l_v)
            q_v = one(V.quantize_mx(T.vq[:], T.vsc[:], T.v_sb[:]))
        spread(i)

    def to_lists(s, x, ready):
        r, d, e, f, gg, o = (T["cr_" + s], T["cd_" + s], T["ce_" + s], T["cf_" + s], T["cg_" + s], T["off_" + s])
        wait(V, "V", *ready)
        a = one(V.transpose(r[:], x[:]))
        wait(V, "V", a)
        a = tok()
        inc(V.tensor_tensor(d[:, 0:16], r[:, 0:16], r[:, 16:32], A.add), a)
        inc(V.tensor_tensor(d[:, 16:32], r[:, 0:16], r[:, 16:32], A.add), a)
        wait(V, "V", a)
        a = one(V.transpose(e[:], d[:]))
        wait(V, "V", a)
        a = one(V.tensor_tensor(f[0:64, :], e[0:64, :], e[64:128, :], A.add))
        wait(V, "V", a)
        a = one(V.tensor_tensor(gg[0:32, :], f[0:32, :], f[32:64, :], A.add))
        wait(V, "V", a)
        a = tok()
        for b in range(4):
            inc(V.tensor_copy(o[32 * b:32 * b + 32, :], gg[0:32, :]), a)
        return a

    la = to_lists("a", T.xa, [xt, c_z])

    wait(V, "V", la, l_v)
    wait(S, "S", la, l_v)

    def gather(i, h, at, engines, tk):
        for t, en in enumerate(engines):
            win = T.v_sb[:, t:2048].indirect(T.off_a[:, 8 * i:8 * i + 8])
            out = h[:, 4 * at + t:4 * at + 512:4]
            if en == "V":
                inc(V.tensor_copy(out, win), tk)
            else:
                inc(S.activation(out, win, F.Copy), tk)

    ga = tok()
    gather(0, T.h_off, 0, "VVSS", ga)
    gather(1, T.h_off, 128, "VVSS", ga)
    gb = tok()
    wait(V, "V", ga)
    q_off = one(V.quantize_mx(T.hq[:, 0:256], T.hsc[:, 0:256], T.h_off[:]))
    gather(2, T.h_on, 0, "VSSV", gb)
    wait(V, "V", gb)
    q_on = one(V.quantize_mx(T.hq[:, 256:384], T.hsc[:, 256:384], T.h_on[:]))

    zs = T.sem["z_in%d" % me]
    zc, zp = T.zq[:, W[me]:W[me] + 128].bitcast(u8), T.zsc[:, W[me]:W[me] + 128]
    wait(g, "g", q_off)
    send([([off[i]], eh[i], T.hq[:, W[i]:W[i] + 128].bitcast(u8), [zc], zs) for i in range(2)])
    send([([off[i]], eh[i], T.hsc[:, W[i]:W[i] + 128], [zp], zs) for i in range(2)])
    wait(g, "g", q_on)
    send([(on, eng_on, T.hq[:, 256:384].bitcast(u8), [zc], zs)])
    send([(on, eng_on, T.hsc[:, 256:384], [zp], zs)])

    wait(V, "V", l_u)
    q_u = one(V.quantize_mx(T.uq[:], T.usc[:], T.u_sb[:]))
    wait(P, "P", q_u, q_v)
    p_v = one(P.matmul_mx(T.ps_v[:], T.uq[:], T.usc[:], T.vq[:], T.vsc[:], True, True))
    y_own = tok()
    wait(S, "S", p_v)
    inc(S.activation(T.yw[:, base_w[me]:base_w[me] + T_K], T.ps_v[:], F.Copy), y_own)

    wait(V, "V", number[me], scanned[me], c_of)
    w0 = tok()
    inc(V.tensor_copy(T.lmi[:, 4 * me:4 * me + 2], T["cm%d" % me][:, T_K - 1:T_K + 1]), w0)
    inc(V.tensor_scalar(T.offs[:, me:me + 1], T["cm%d" % me][:, T_K:T_K + 1], float(base_w[me]), None, A.add), w0)
    wait(V, "V", w0, far(T.sem.mi_in, sum(len(eng_on) if q in on else half for q in others)))
    w1 = tok()
    inc(V.tensor_reduce(T.wm[:, 0:1], T.lmi[:, 0:16:4], AxisListType.X, A.max), w1)
    inc(V.tensor_tensor(T.gn[:], T.lmi[:, 1:16:4], T.base4[:], A.add), w1)
    wait(V, "V", w1)
    w2 = one(V.tensor_scalar(T.pen[:], T.lmi[:, 0:16:4], T.wm[:, 0:1], FAR, A.is_lt, A.mult))
    wait(V, "V", w2)
    w3 = tok()
    inc(V.tensor_tensor(T.cano[:], T.pen[:], T.offs[:], A.add), w3)
    inc(V.tensor_tensor(T.cand[:], T.pen[:], T.gn[:], A.add), w3)
    wait(V, "V", w3)
    w4 = one(V.tensor_reduce(T.osel[:, 0:1], T.cano[:], AxisListType.X, A.min))
    w5 = one(V.tensor_reduce(T.winr[:, 0:1], T.cand[:], AxisListType.X, A.min))
    wait(Y, "Y", w5)
    out_w = one(Y.dma_start(T.win[:], T.winr[:, 0:1]), 16)
    wait(V, "V", w4)
    w6 = one(V.tensor_scalar(T.xb[:, 0:8], T.hm[:], T.osel[:, 0:1], None, A.mult))
    lb = to_lists("b", T.xb, [w6])

    y_oth = tok()
    y_last = tok()
    for i, q in enumerate(off + on):
        wait(P, "P", far(T.sem["z_in%d" % q], 2 * (len(eng_on) if q in on else half)))
        p = one(P.matmul_mx(T["ps_y%d" % i][:, 0:128], T.uq[:], T.usc[:], T.zq[:, W[q]:W[q] + 128],
                            T.zsc[:, W[q]:W[q] + 128], True, True))
        dst, src = T.yw[:, base_w[q]:base_w[q] + 128], T["ps_y%d" % i][:, 0:128]
        if i == 1:
            wait(S, "S", p)
            inc(S.activation(dst, src, F.Copy), y_oth)
        else:
            wait(V, "V", p)
            inc(V.tensor_copy(dst, src), y_last)
    wait(V, "V", lb, y_own, y_oth, y_last)
    fin = one(V.tensor_copy(T.ysb[:], T.yw[:].indirect(T.off_b[:, 0:8])))
    wait(Y, "Y", fin)
    out_y = one(Y.dma_start(T.y[:], T.ysb[:]), 16)
    wait(Y, "Y", out_w, out_y)
    g.wait_ge(T.sem.sent, sent[0])
